import numpy as np
import ml_dtypes


def mxq(x, axis, fmt="e4m3"):
    dtype, down = {"e4m3": (ml_dtypes.float8_e4m3fn, 7), "e5m2": (ml_dtypes.float8_e5m2, 14)}[fmt]
    v = np.moveaxis(np.asarray(x, np.float32).astype(ml_dtypes.bfloat16).astype(np.float64), axis, -1)
    blocks = v.reshape(v.shape[:-1] + (-1, 32))
    amax = np.abs(blocks).max(-1, keepdims=True)
    byte = np.maximum(np.where(amax > 0, np.frexp(amax)[1] - 1 + 127, 0) - down, 1)
    scale = np.exp2(byte - 127.0)
    codes = (blocks / scale).astype(np.float32).astype(dtype).astype(np.float64)
    return np.moveaxis((codes * scale).reshape(v.shape), -1, axis)


WIDE = False


def mx_kscale(k):
    if not WIDE:
        return np.ones(k)
    levels = np.array([10, -10, 5, -5, 0])
    if k % 512:
        return np.exp2(np.random.permutation(np.resize(levels, k // 32))).repeat(32)
    a = np.empty((k // 512, 16))
    for p in range(k // 512):
        a[p, :8] = np.random.permutation(np.resize(levels, 8))
        for g in range(8):
            far = levels[np.abs(levels - a[p, g]) >= 10]
            a[p, g + 8] = far[np.random.randint(len(far))]
    return np.exp2(a.ravel()).repeat(32)


def f64(x):
    return np.asarray(x).astype(np.float64)


def striped(idx):
    return np.tile(idx.reshape(-1, 16).T, (8, 1)).astype(np.uint16)


def unstriped(offs):
    return offs[:16].T.reshape(-1).astype(np.int64)


E2M1 = np.array([0.0, 0.5, 1.0, 1.5, 2.0, 3.0, 4.0, 6.0, -0.0, -0.5, -1.0, -1.5, -2.0, -3.0, -4.0, -6.0])


def pack_weight(w, fmt):
    k, n = w.shape
    w = f64(np.asarray(w, np.float32).astype(ml_dtypes.bfloat16)).reshape(k // 32, 32, n)
    amax = np.abs(w).max(1)
    if fmt == "e4m3":
        byte = np.frexp(amax)[1] - 1 + 127 - 7
    else:
        mant, ex = np.frexp(amax / 6.0)
        byte = np.where(mant > 0.5, ex, ex - 1) + 127
    byte = np.clip(np.where(amax > 0, byte, 1), 1, 254)
    scaled = (w * np.exp2(127.0 - byte)[:, None, :]).reshape(k, n).astype(np.float32)
    by_word = np.ascontiguousarray(scaled.reshape(k // 512, 128, 4, n).transpose(0, 1, 3, 2))
    if fmt == "e4m3":
        words = by_word.astype(ml_dtypes.float8_e4m3fn).view(np.uint8)
    else:
        c = by_word.astype(ml_dtypes.float4_e2m1fn).view(np.uint8) & 0xF
        words = (c[..., 0::2] | (c[..., 1::2] << 4)).reshape(k // 512, 128, 2 * n)
    return np.ascontiguousarray(words), np.ascontiguousarray(byte.astype(np.uint8).reshape(k // 512, 16, n))


def unpack_weight(words, scales, fmt):
    g, _, n = scales.shape
    words = np.ascontiguousarray(words).reshape(g, 128, n, -1)
    if fmt == "e4m3":
        vals = words.view(ml_dtypes.float8_e4m3fn).astype(np.float64)
    else:
        nib = np.empty((g, 128, n, 4), np.uint8)
        nib[..., 0::2] = words & 0xF
        nib[..., 1::2] = words >> 4
        vals = E2M1[nib]
    vals = vals * np.repeat(np.exp2(scales.astype(np.float64) - 127.0), 8, axis=1)[..., None]
    return vals.transpose(0, 1, 3, 2).reshape(g * 512, n)


def gelu(v):
    return 0.5 * v * (1.0 + np.tanh(np.sqrt(2.0 / np.pi) * (v + 0.044715 * v**3)))


def striped8(idx):
    return np.concatenate([v.reshape(-1, 16).T for v in idx]).astype(np.uint16)


def unstriped8(offs):
    return np.stack([offs[16 * g:16 * g + 16].T.reshape(-1) for g in range(8)]).astype(np.int64)


def heads(h, wgt, idx8):
    r = np.arange(h.shape[0])
    return wgt[r // 4 % 128] * h[r[:, None], idx8[r % 512 // 64]]


def put_heads(h, wgs, idx8, t2):
    r = np.arange(h.shape[0])
    page = np.zeros((h.shape[0], t2))
    page[r[:, None], idx8[r % 512 // 64]] = wgs[r // 4 % 128] * h
    return page


K, H, N, T, S, P, T2 = 512, 1024, 640, 4096, 1024, 1024, 2048


def setup_inputs():
    n = np.random.standard_normal
    s = mx_kscale(K)[:, None]
    u = mx_kscale(H)[:, None]
    d = {}
    d["tab_words"], d["tab_scales"] = pack_weight(n((K, T)) * s, "e4m3")
    d["offs"] = striped(np.random.permutation(T)[:S])
    d["offs2"] = striped8(np.stack([np.random.permutation(T2)[:S] for _ in range(8)]))
    d["offs3"] = striped8(np.stack([np.random.permutation(T2)[:P] for _ in range(8)]))
    d["w1"] = (n((K, H)) / s / K**0.5).astype(np.float32)
    d["w2_words"], d["w2_scales"] = pack_weight(1.5 * n((K, H)) / s / K**0.5, "e2m1")
    d["gain"] = (np.exp(0.3 * n(H)) * u[:, 0]).astype(np.float32)
    d["wgs"] = np.repeat(np.random.uniform(0.5, 2.0, (8, S)), 16, axis=0).astype(np.float32)
    d["wgt"] = np.repeat(np.random.uniform(0.5, 2.0, (8, P)), 16, axis=0).astype(np.float32)
    d["light"] = (n((H, P)) * u).astype(np.float32)
    d["w3_words"], d["w3_scales"] = pack_weight(n((H, N)) / u / H**0.5, "e4m3")
    d["w4"] = (n((H, N)) / u / H**0.5).astype(np.float32)
    return d


def reference(tab_words, tab_scales, offs, offs2, offs3, w1, w2_words, w2_scales, gain, wgs, wgt, light, w3_words, w3_scales, w4):
    v = unpack_weight(tab_words, tab_scales, "e4m3")[:, unstriped(offs)]
    a = mxq(f64(w1), 0, "e4m3").T @ v
    b = unpack_weight(w2_words, w2_scales, "e2m1").T @ v
    h = np.maximum(a, np.tanh(b)) * f64(gain)[:, None]
    page = put_heads(h, f64(wgs), unstriped8(offs2), T2)
    x = heads(page, f64(wgt), unstriped8(offs3))
    z = mxq(np.abs(x - f64(light)), 0, "e4m3")
    y = unpack_weight(w3_words, w3_scales, "e4m3").T @ z
    y2 = mxq(f64(w4), 0, "e4m3").T @ z
    return y / (1.0 + np.abs(y2))

@@ -1,0 +1,373 @@
+from contextlib import ExitStack
+
+import concourse.mybir as mybir
+from concourse.masks import make_identity
+
+K, H, N, T, S, M, T2 = 512, 1024, 640, 4096, 1024, 1024, 2048
+FLOPS = 2 * (2 * K * H * S + 2 * H * N * M)
+
+F32 = mybir.dt.float32
+BF16 = mybir.dt.bfloat16
+I32 = mybir.dt.int32
+U32 = mybir.dt.uint32
+U16 = mybir.dt.uint16
+U8 = mybir.dt.uint8
+FP8X4 = mybir.dt.float8_e4m3fn_x4
+FP4X4 = mybir.dt.float4_e2m1fn_x4
+ALU = mybir.AluOpType
+ACT = mybir.ActivationFunctionType
+
+P = 128
+PACK = 4
+K_PASS = P * PACK
+HALF = 512
+CHUNK = 256
+CHUNKS = M // CHUNK
+GROUPS = ((0, 1), (2, 3), (4,))
+STEPS = 2 * PACK * 2
+
+
+def tile_list_pelt_round_scores_kernel(
+    tc, tab_words, tab_scales, offs, offs2, offs3, w1, w2_words, w2_scales, gain, wgs, wgt, light,
+    w3_words, w3_scales, w4, out,
+):
+    nc = tc.nc
+    with ExitStack() as ctx:
+        lists = ctx.enter_context(tc.tile_pool(name="lists", bufs=1))
+        keep = ctx.enter_context(tc.tile_pool(name="keep", bufs=1))
+        ring = ctx.enter_context(tc.tile_pool(name="ring", bufs=3))
+        psum = ctx.enter_context(tc.psum_pool(name="psum", bufs=2))
+
+        def held(shape, dtype, name, tag=None):
+            return keep.tile(shape, dtype, name=name, tag=tag or name, align_bytes=64)
+
+        def load_scale_rows(engine, plane, rows):
+            for q in range(4):
+                engine.dma_start(
+                    out=plane[32 * q : 32 * q + 4].bitcast(I32),
+                    in_=rows[:, 4 * q : 4 * q + 4, :].rearrange("a r c -> r a c").bitcast(I32),
+                )
+
+        tab_s = held([P, 1, T], U8, "tab_s", "tab_s")
+        nc.vector.memset(tab_s[:].bitcast(I32), 0)
+        w2_s_raw = held([P, 1, H], U8, "w2_s_raw", "w2_s_raw")
+        nc.gpsimd.memset(w2_s_raw[:].bitcast(I32), 0)
+        load_scale_rows(nc.gpsimd, w2_s_raw, w2_scales)
+
+        idx = lists.tile([P, S // 16], U16, name="idx")
+        nc.sync.dma_start(idx[:], offs)
+        idx2 = lists.tile([P, S // 16], U16, name="idx2")
+        nc.sync.dma_start(idx2[:], offs2)
+        idx3 = lists.tile([P, M // 16], U16, name="idx3")
+        nc.sync.dma_start(idx3[:], offs3)
+        w2_raw = held([P, 2 * H], U8, "w2_raw", "w2_raw")
+        nc.sync.dma_start(out=w2_raw[:].bitcast(I32), in_=w2_words[0].bitcast(I32))
+
+        w1_q = [held([P, K_PASS], U32, "w1_q%d" % b) for b in range(2)]
+        w1_s = [held([P, K_PASS], U8, "w1_s%d" % b) for b in range(2)]
+
+        def load_w1(b):
+            raw = held([P, PACK, K_PASS], F32, "w1_raw%d" % b, "w_raw")
+            nc.sync.dma_start(
+                out=raw[:], in_=w1[:, b * K_PASS : (b + 1) * K_PASS].rearrange("(p j) c -> p j c", j=PACK)
+            )
+            return raw
+
+        def quantize_w1(b, raw):
+            rounded = held([P, PACK * K_PASS], BF16, "w1_bf%d" % b, "w1_bf")
+            nc.scalar.copy(
+                out=rounded[:].rearrange("p (t m j) -> p m j t", t=PACK, j=PACK),
+                in_=raw[:].rearrange("p j (m t) -> p m j t", t=PACK),
+            )
+            nc.vector.quantize_mx(out=w1_q[b][:].bitcast(FP8X4), scales=w1_s[b][:], in_=rounded[:])
+
+        w1_raw0 = load_w1(0)
+        tab_w = held([P, T], I32, "tab_w", "big")
+        nc.sync.dma_start(out=tab_w[:], in_=tab_words[0].rearrange("p t i -> p (t i)").bitcast(I32))
+        load_scale_rows(nc.scalar, tab_s, tab_scales)
+
+        pages = [held([P, T2], F32, "page%d" % t) for t in range(2)]
+        for page in pages:
+            nc.vector.memset(page[:], 0.0)
+
+        w2_q = held([P, 2 * H], U8, "w2_q")
+        for b in range(2):
+            cols = slice(b * H, (b + 1) * H)
+            nc.vector.tensor_copy(
+                out=w2_q[:, cols].bitcast(U16).rearrange("p (t m) -> p t m", t=PACK),
+                in_=w2_raw[:, cols].bitcast(U16).rearrange("p (m t) -> p t m", t=PACK),
+            )
+        w2_s = held([P, H], U8, "w2_s")
+        nc.vector.tensor_copy(
+            out=w2_s[:].rearrange("p (b t m) -> p b t m", b=2, t=PACK),
+            in_=w2_s_raw[:, 0, :].rearrange("p (b m t) -> p b t m", b=2, t=PACK),
+        )
+        factors = held([P, S + 2 * PACK], F32, "factors", "w2_raw")
+        wgs_sb = factors[:, :S]
+        gain_sb = factors[:, S:].rearrange("p (b t) -> p b t", b=2)
+        nc.sync.dma_start(out=gain_sb, in_=gain.rearrange("(b p t) -> p b t", b=2, t=PACK))
+        nc.sync.dma_start(out=wgs_sb, in_=wgs)
+
+        quantize_w1(0, w1_raw0)
+        v_s = [held([P, HALF], U8, "v_s%d" % half) for half in range(2)]
+        v_q = [held([P, HALF], U32, "v_q%d" % half) for half in range(2)]
+        for half in range(2):
+            entries = idx[:, half * HALF // 16 : (half + 1) * HALF // 16]
+            nc.vector.tensor_copy(v_s[half][:], tab_s[:, 0, :].indirect(entries))
+            nc.vector.tensor_copy(v_q[half][:], tab_w[:].bitcast(U32).indirect(entries))
+        for t, tag in ((2, "tab_s"), (3, "big")):
+            pages.append(held([P, T2], F32, "page%d" % t, tag))
+            nc.gpsimd.memset(pages[t][:], 0.0)
+
+        identity = held([P, P], F32, "identity")
+        make_identity(nc, identity[:])
+
+        wgt_neg = held([P, M], F32, "wgt_neg")
+        w4_q = held([P, 2 * N], U32, "w4_q")
+        w4_s = held([P, 2 * N], U8, "w4_s")
+        w4_bf = held([P, 2 * N * PACK], BF16, "w4_bf")
+        w3_s = held([P, 2, N], U8, "w3_s")
+        light_sb = {}
+
+        def load_light(b):
+            light_sb[b] = held([P, PACK, M], F32, "light%d" % b, "w_raw")
+            nc.sync.dma_start(
+                out=light_sb[b][:], in_=light[b * K_PASS : (b + 1) * K_PASS, :].rearrange("(p t) m -> p t m", t=PACK)
+            )
+
+        def prepare_wgt():
+            raw = held([P, M], F32, "wgt_raw", "w2_s_raw")
+            nc.sync.dma_start(out=raw[:], in_=wgt)
+            nc.scalar.mul(wgt_neg[:], raw[:], -1.0)
+
+        def prepare_w1b():
+            quantize_w1(1, load_w1(1))
+
+        def round_w4(a):
+            raw = held([P, PACK, N], F32, "w4_raw%d" % a, "w_raw")
+            nc.sync.dma_start(
+                out=raw[:], in_=w4[a * K_PASS : (a + 1) * K_PASS, :].rearrange("(p j) c -> p j c", j=PACK)
+            )
+            nc.scalar.copy(
+                out=w4_bf[:, a * N * PACK : (a + 1) * N * PACK].rearrange("p (c i j) -> p c j i", i=4, j=PACK),
+                in_=raw[:].rearrange("p j (c i) -> p c j i", i=4),
+            )
+
+        def quantize_w4():
+            for lo, hi in ((0, 1024), (1024, 2 * N)):
+                nc.vector.quantize_mx(
+                    out=w4_q[:, lo:hi].bitcast(FP8X4), scales=w4_s[:, lo:hi], in_=w4_bf[:, PACK * lo : PACK * hi]
+                )
+
+        w3 = {}
+
+        def load_w3():
+            w3_q = held([P, 2, N], I32, "w3_q", "w2_s_raw")
+            w3["q"] = w3_q
+            nc.sync.dma_start(out=w3_q[:], in_=w3_words.rearrange("a p c i -> p a (c i)").bitcast(I32))
+            nc.gpsimd.memset(w3_s[:].bitcast(I32), 0)
+            load_scale_rows(nc.sync, w3_s, w3_scales)
+
+        def place(k):
+            return k // (2 * PACK), k // 2 % PACK, k % 2
+
+        made = {}
+
+        def products(k):
+            b, t, half = place(k)
+            cols = slice(t * P, (t + 1) * P)
+            entries = slice(half * HALF, (half + 1) * HALF)
+            sum_b = psum.tile([P, HALF], F32, name="sum_b", tag="B")
+            c2 = b * K_PASS + t * P
+            nc.tensor.matmul_mx(
+                out=sum_b[:], lhsT=w2_q[:, 2 * c2 : 2 * (c2 + P)].bitcast(FP4X4), lhsT_scale=w2_s[:, c2 : c2 + P],
+                rhs=v_q[half][:].bitcast(FP8X4), rhs_scale=v_s[half][:], start=True, stop=True,
+            )
+            sum_a = psum.tile([P, HALF], F32, name="sum_a", tag="A")
+            nc.tensor.matmul_mx(
+                out=sum_a[:], lhsT=w1_q[b][:, cols].bitcast(FP8X4), lhsT_scale=w1_s[b][:, cols],
+                rhs=v_q[half][:].bitcast(FP8X4), rhs_scale=v_s[half][:], start=True, stop=True,
+            )
+            tanh_b = ring.tile([P, HALF], F32, name="tanh_b")
+            nc.scalar.activation(out=tanh_b[:], in_=sum_b[:], func=ACT.Tanh)
+            weight = ring.tile([P, HALF], F32, name="weight")
+            nc.scalar.activation(out=weight[:], in_=wgs_sb[:, entries], func=ACT.Copy, scale=gain_sb[:, b, t : t + 1])
+            made[k] = (sum_a, tanh_b, weight)
+
+        larger = {}
+
+        def maximum(k):
+            sum_a, tanh_b, weight = made[k]
+            larger[k] = ring.tile([P, HALF], F32, name="larger")
+            nc.vector.tensor_tensor(larger[k][:], sum_a[:], tanh_b[:], ALU.max)
+
+        def scatter(k):
+            b, t, half = place(k)
+            nc.vector.tensor_tensor(
+                pages[t][:].indirect(idx2[:, half * HALF // 16 : (half + 1) * HALF // 16]),
+                larger[k][:], made[k][2][:], ALU.mult,
+            )
+
+        x_first = {}
+
+        def gather_first(t):
+            x_first[t] = keep.tile([P, M], F32, name="x_first%d" % t, tag="x%d" % t, align_bytes=64)
+            nc.vector.tensor_tensor(x_first[t][:], pages[t][:].indirect(idx3[:]), wgt_neg[:], ALU.mult)
+
+        z0_q = held([P, M], U32, "z0_q")
+        z0_s = held([P, M], U8, "z0_s")
+
+        def distance_first(c):
+            back = psum.tile([P, 2, CHUNK], F32, name="back", tag="R")
+            for u in range(2):
+                turned = psum.tile([P, 2, 2, P], F32, name="turned", tag="F")
+                blocks = [(a, e) for a in range(2) for e in range(2)]
+                for n, (a, e) in enumerate(blocks):
+                    cols = slice(c * CHUNK + a * P, c * CHUNK + (a + 1) * P)
+                    nc.tensor.matmul(
+                        turned[:, a, e, :], light_sb[0][:, 2 * u + e, cols], identity[:],
+                        start=(n == 0), stop=False, is_transpose=True,
+                    )
+                for n, (a, e) in enumerate(blocks):
+                    cols = slice(c * CHUNK + a * P, c * CHUNK + (a + 1) * P)
+                    nc.tensor.matmul(
+                        turned[:, a, e, :], x_first[2 * u + e][:, cols], identity[:],
+                        start=False, stop=(n == len(blocks) - 1), is_transpose=True,
+                    )
+                pairs = ring.tile([P, 2, P, 2], BF16, name="pairs")
+                nc.scalar.activation(out=pairs[:], in_=turned[:].rearrange("m a e p -> m a p e"), func=ACT.Abs)
+                words = pairs[:].rearrange("m a p e -> m (a p e)").bitcast(F32)
+                for a in range(2):
+                    nc.tensor.transpose(back[:, u, a * P : (a + 1) * P], words[:, a * P : (a + 1) * P], identity[:])
+            z_words = ring.tile([P, CHUNK, 2], F32, name="z_words", align_bytes=64)
+            nc.scalar.copy(out=z_words[:], in_=back[:].rearrange("p u m -> p m u"))
+            return z_words
+
+        def quantize_first(c, z_words):
+            cols = slice(c * CHUNK, (c + 1) * CHUNK)
+            nc.vector.quantize_mx(
+                out=z0_q[:, cols].bitcast(FP8X4), scales=z0_s[:, cols],
+                in_=z_words[:].rearrange("p m u -> p (m u)").bitcast(BF16),
+            )
+
+        side_jobs = {
+            0: prepare_wgt, 1: prepare_w1b, 2: lambda: round_w4(0), 3: load_w3,
+            4: lambda: round_w4(1), 5: lambda: load_light(0), 7: quantize_w4,
+        }
+        z_first = {}
+        products(0)
+        products(1)
+        maximum(0)
+        for k in range(STEPS):
+            if k + 2 < STEPS:
+                products(k + 2)
+            if k + 1 < STEPS:
+                maximum(k + 1)
+            if k % 2 == 0 and 2 <= k <= 2 * PACK:
+                gather_first(k // 2 - 1)
+            scatter(k)
+            if k in side_jobs:
+                side_jobs[k]()
+            c = k - (2 * PACK + 1)
+            if 0 <= c < CHUNKS:
+                z_first[c] = distance_first(c)
+            if 0 <= c - 1 < CHUNKS:
+                quantize_first(c - 1, z_first[c - 1])
+            if c == CHUNKS - 1:
+                load_light(1)
+
+        x_second = {}
+
+        def gather_second(c, t):
+            if t == 0:
+                x_second[c] = keep.tile([P, PACK, CHUNK], F32, name="x_second", tag="x%d" % c, align_bytes=64)
+            nc.vector.tensor_tensor(
+                x_second[c][:, t, :], pages[t][:].indirect(idx3[:, c * CHUNK // 16 : (c + 1) * CHUNK // 16]),
+                wgt_neg[:, c * CHUNK : (c + 1) * CHUNK], ALU.mult,
+            )
+
+        z_second = {}
+
+        def distance_second(c):
+            diff = ring.tile([P, PACK, CHUNK], BF16, name="diff")
+            nc.vector.tensor_tensor(diff[:], x_second[c][:], light_sb[1][:, :, c * CHUNK : (c + 1) * CHUNK], ALU.add)
+            z_second[c] = ring.tile([P, CHUNK * PACK], BF16, name="z_second", align_bytes=64)
+            nc.scalar.activation(
+                out=z_second[c][:].rearrange("p (c i t) -> p c t i", i=4, t=PACK),
+                in_=diff[:].rearrange("p t (c i) -> p c t i", i=4), func=ACT.Abs,
+            )
+
+        z1 = {}
+
+        def quantize_second(c):
+            z1_q = ring.tile([P, CHUNK], U32, name="z1_q", align_bytes=64)
+            z1_s = ring.tile([P, CHUNK], U8, name="z1_s", align_bytes=64)
+            nc.vector.quantize_mx(out=z1_q[:].bitcast(FP8X4), scales=z1_s[:], in_=z_second[c][:])
+            z1[c] = (z1_q, z1_s)
+
+        scored = {}
+
+        def score(c, g):
+            tiles = GROUPS[g]
+            cols = slice(c * CHUNK, (c + 1) * CHUNK)
+            turn = (c * len(GROUPS) + g) % 2
+            y2 = psum.tile([P, len(tiles), CHUNK], F32, name="y2", tag="BR"[turn])
+            y = psum.tile([P, len(tiles), CHUNK], F32, name="y", tag="AF"[turn])
+            moving = ((z0_q[:, cols], z0_s[:, cols]), (z1[c][0][:], z1[c][1][:]))
+            for i, nt in enumerate(tiles):
+                for a in range(2):
+                    wc = slice(a * N + nt * P, a * N + (nt + 1) * P)
+                    nc.tensor.matmul_mx(
+                        out=y2[:, i, :], lhsT=w4_q[:, wc].bitcast(FP8X4), lhsT_scale=w4_s[:, wc],
+                        rhs=moving[a][0].bitcast(FP8X4), rhs_scale=moving[a][1], start=(a == 0), stop=(a == 1),
+                    )
+            for i, nt in enumerate(tiles):
+                for a in range(2):
+                    wc = slice(nt * P, (nt + 1) * P)
+                    nc.tensor.matmul_mx(
+                        out=y[:, i, :], lhsT=w3["q"][:, a, wc].bitcast(FP8X4), lhsT_scale=w3_s[:, a, wc],
+                        rhs=moving[a][0].bitcast(FP8X4), rhs_scale=moving[a][1], start=(a == 0), stop=(a == 1),
+                    )
+            size = ring.tile([P, len(tiles), CHUNK], F32, name="size", bufs=2)
+            nc.scalar.activation(out=size[:], in_=y2[:], func=ACT.Abs)
+            root = ring.tile([P, len(tiles), CHUNK], F32, name="root", bufs=2)
+            nc.scalar.activation(out=root[:], in_=size[:], func=ACT.Abs_reciprocal_sqrt, bias=1.0)
+            inverse = ring.tile([P, len(tiles), CHUNK], F32, name="inverse")
+            nc.scalar.activation(out=inverse[:], in_=root[:], func=ACT.Square)
+            scored[c, g] = (y, inverse)
+
+        def finish(c, g):
+            tiles = GROUPS[g]
+            y, inverse = scored[c, g]
+            result = ring.tile([P, len(tiles), CHUNK], F32, name="result")
+            nc.vector.tensor_tensor(result[:], y[:], inverse[:], ALU.mult)
+            nc.sync.dma_start(
+                out=out[tiles[0] * P : (tiles[-1] + 1) * P, c * CHUNK : (c + 1) * CHUNK].rearrange("(i p) m -> p i m", p=P),
+                in_=result[:],
+            )
+
+        for t in range(PACK):
+            gather_second(0, t)
+        distance_second(0)
+        gather_second(1, 0)
+        gather_second(1, 1)
+        for c in range(CHUNKS):
+            quantize_second(c)
+            score(c, 0)
+            if c > 0:
+                finish(c - 1, 1)
+            if c + 1 < CHUNKS:
+                gather_second(c + 1, 2)
+                gather_second(c + 1, 3)
+            if c > 0:
+                finish(c - 1, 2)
+            if c + 1 < CHUNKS:
+                distance_second(c + 1)
+            score(c, 1)
+            score(c, 2)
+            finish(c, 0)
+            if c + 2 < CHUNKS:
+                gather_second(c + 2, 0)
+                gather_second(c + 2, 1)
+        finish(CHUNKS - 1, 1)
+        finish(CHUNKS - 1, 2)

@@ -25,6 +25,10 @@ CHUNK = 256
 CHUNKS = M // CHUNK
 GROUPS = ((0, 1), (2, 3), (4,))
 STEPS = 2 * PACK * 2
+W1_ON_VECTOR = 48
+SQUARED_CHUNKS = 2
+WIDTHS = (128, 256, 256, 256, 128)
+STARTS = [sum(WIDTHS[:c]) for c in range(len(WIDTHS))]
 
 
 def tile_list_pelt_round_scores_kernel(
@@ -66,24 +70,28 @@ def tile_list_pelt_round_scores_kernel(
         w1_q = [held([P, K_PASS], U32, "w1_q%d" % b) for b in range(2)]
         w1_s = [held([P, K_PASS], U8, "w1_s%d" % b) for b in range(2)]
 
-        def load_w1(b):
-            raw = held([P, PACK, K_PASS], F32, "w1_raw%d" % b, "w_raw")
-            nc.sync.dma_start(
-                out=raw[:], in_=w1[:, b * K_PASS : (b + 1) * K_PASS].rearrange("(p j) c -> p j c", j=PACK)
-            )
+        def load_rows(flat, rows):
+            raw = flat.rearrange("p (j c) -> p j c", j=PACK)
+            nc.sync.dma_start(out=raw, in_=rows.rearrange("(p j) c -> p j c", j=PACK))
             return raw
 
-        def quantize_w1(b, raw):
-            rounded = held([P, PACK * K_PASS], BF16, "w1_bf%d" % b, "w1_bf")
-            nc.scalar.copy(
-                out=rounded[:].rearrange("p (t m j) -> p m j t", t=PACK, j=PACK),
-                in_=raw[:].rearrange("p j (m t) -> p m j t", t=PACK),
-            )
-            nc.vector.quantize_mx(out=w1_q[b][:].bitcast(FP8X4), scales=w1_s[b][:], in_=rounded[:])
+        def quantize_w1(b, raw, on_vector):
+            rounded = held([P, PACK * K_PASS], BF16, "w1_bf%d" % b)
+            dealt = rounded[:].rearrange("p (t m j) -> p m j t", t=PACK, j=PACK)
+            source = raw.rearrange("p j (m t) -> p m j t", t=PACK)
+            nc.scalar.copy(out=dealt[:, on_vector:], in_=source[:, on_vector:])
+            if on_vector:
+                nc.vector.tensor_copy(out=dealt[:, :on_vector], in_=source[:, :on_vector])
+            for cols in (slice(0, 2 * P), slice(2 * P, 4 * P)):
+                nc.vector.quantize_mx(
+                    out=w1_q[b][:, cols].bitcast(FP8X4), scales=w1_s[b][:, cols],
+                    in_=rounded[:, PACK * cols.start : PACK * cols.stop],
+                )
 
-        w1_raw0 = load_w1(0)
         tab_w = held([P, T], I32, "tab_w", "big")
-        nc.sync.dma_start(out=tab_w[:], in_=tab_words[0].rearrange("p t i -> p (t i)").bitcast(I32))
+        for cols in (slice(0, T // 2), slice(T // 2, T)):
+            nc.sync.dma_start(out=tab_w[:, cols], in_=tab_words[0].rearrange("p t i -> p (t i)").bitcast(I32)[:, cols])
+        w1_raw0 = load_rows(held([P, PACK * K_PASS], F32, "w1_raw0", "late")[:], w1[:, :K_PASS])
         load_scale_rows(nc.scalar, tab_s, tab_scales)
 
         pages = [held([P, T2], F32, "page%d" % t) for t in range(2)]
@@ -108,13 +116,14 @@ def tile_list_pelt_round_scores_kernel(
         nc.sync.dma_start(out=gain_sb, in_=gain.rearrange("(b p t) -> p b t", b=2, t=PACK))
         nc.sync.dma_start(out=wgs_sb, in_=wgs)
 
-        quantize_w1(0, w1_raw0)
         v_s = [held([P, HALF], U8, "v_s%d" % half) for half in range(2)]
         v_q = [held([P, HALF], U32, "v_q%d" % half) for half in range(2)]
-        for half in range(2):
-            entries = idx[:, half * HALF // 16 : (half + 1) * HALF // 16]
-            nc.vector.tensor_copy(v_s[half][:], tab_s[:, 0, :].indirect(entries))
-            nc.vector.tensor_copy(v_q[half][:], tab_w[:].bitcast(U32).indirect(entries))
+        for gathered, window in ((v_s, tab_s[:, 0, :]), (v_q, tab_w[:].bitcast(U32))):
+            for half in range(2):
+                nc.vector.tensor_copy(
+                    gathered[half][:], window.indirect(idx[:, half * HALF // 16 : (half + 1) * HALF // 16])
+                )
+        quantize_w1(0, w1_raw0, W1_ON_VECTOR)
         for t, tag in ((2, "tab_s"), (3, "big")):
             pages.append(held([P, T2], F32, "page%d" % t, tag))
             nc.gpsimd.memset(pages[t][:], 0.0)
@@ -122,35 +131,29 @@ def tile_list_pelt_round_scores_kernel(
         identity = held([P, P], F32, "identity")
         make_identity(nc, identity[:])
 
-        wgt_neg = held([P, M], F32, "wgt_neg")
+        sizes = [M, PACK * K_PASS, PACK * M, PACK * N, PACK * N, PACK * M]
+        late = held([P, sum(sizes)], F32, "late", "late")
+        parts = [late[:, sum(sizes[:n]) : sum(sizes[: n + 1])] for n in range(len(sizes))]
+        wgt_neg = parts[0]
+        nc.sync.dma_start(out=wgt_neg, in_=wgt)
+        w1_raw1 = load_rows(parts[1], w1[:, K_PASS:])
+        light_sb = [load_rows(parts[2], light[:K_PASS, :])]
+        w4_raw = [load_rows(parts[3 + a], w4[a * K_PASS : (a + 1) * K_PASS, :]) for a in range(2)]
+        light_sb.append(load_rows(parts[5], light[K_PASS:, :]))
+        w3_q = held([P, 2, N], I32, "w3_q", "w1_bf0")
+        nc.sync.dma_start(out=w3_q[:], in_=w3_words.rearrange("a p c i -> p a (c i)").bitcast(I32))
+        w3_s = held([P, 2, N], U8, "w3_s", "w2_s_raw")
+        nc.gpsimd.memset(w3_s[:].bitcast(I32), 0)
+        load_scale_rows(nc.sync, w3_s, w3_scales)
+
         w4_q = held([P, 2 * N], U32, "w4_q")
         w4_s = held([P, 2 * N], U8, "w4_s")
         w4_bf = held([P, 2 * N * PACK], BF16, "w4_bf")
-        w3_s = held([P, 2, N], U8, "w3_s")
-        light_sb = {}
-
-        def load_light(b):
-            light_sb[b] = held([P, PACK, M], F32, "light%d" % b, "w_raw")
-            nc.sync.dma_start(
-                out=light_sb[b][:], in_=light[b * K_PASS : (b + 1) * K_PASS, :].rearrange("(p t) m -> p t m", t=PACK)
-            )
-
-        def prepare_wgt():
-            raw = held([P, M], F32, "wgt_raw", "w2_s_raw")
-            nc.sync.dma_start(out=raw[:], in_=wgt)
-            nc.scalar.mul(wgt_neg[:], raw[:], -1.0)
-
-        def prepare_w1b():
-            quantize_w1(1, load_w1(1))
 
         def round_w4(a):
-            raw = held([P, PACK, N], F32, "w4_raw%d" % a, "w_raw")
-            nc.sync.dma_start(
-                out=raw[:], in_=w4[a * K_PASS : (a + 1) * K_PASS, :].rearrange("(p j) c -> p j c", j=PACK)
-            )
             nc.scalar.copy(
                 out=w4_bf[:, a * N * PACK : (a + 1) * N * PACK].rearrange("p (c i j) -> p c j i", i=4, j=PACK),
-                in_=raw[:].rearrange("p j (c i) -> p c j i", i=4),
+                in_=w4_raw[a].rearrange("p j (c i) -> p c j i", i=4),
             )
 
         def quantize_w4():
@@ -158,15 +161,6 @@ def tile_list_pelt_round_scores_kernel(
                 nc.vector.quantize_mx(
                     out=w4_q[:, lo:hi].bitcast(FP8X4), scales=w4_s[:, lo:hi], in_=w4_bf[:, PACK * lo : PACK * hi]
                 )
-
-        w3 = {}
-
-        def load_w3():
-            w3_q = held([P, 2, N], I32, "w3_q", "w2_s_raw")
-            w3["q"] = w3_q
-            nc.sync.dma_start(out=w3_q[:], in_=w3_words.rearrange("a p c i -> p a (c i)").bitcast(I32))
-            nc.gpsimd.memset(w3_s[:].bitcast(I32), 0)
-            load_scale_rows(nc.sync, w3_s, w3_scales)
 
         def place(k):
             return k // (2 * PACK), k // 2 % PACK, k % 2
@@ -176,7 +170,6 @@ def tile_list_pelt_round_scores_kernel(
         def products(k):
             b, t, half = place(k)
             cols = slice(t * P, (t + 1) * P)
-            entries = slice(half * HALF, (half + 1) * HALF)
             sum_b = psum.tile([P, HALF], F32, name="sum_b", tag="B")
             c2 = b * K_PASS + t * P
             nc.tensor.matmul_mx(
@@ -190,29 +183,40 @@ def tile_list_pelt_round_scores_kernel(
             )
             tanh_b = ring.tile([P, HALF], F32, name="tanh_b")
             nc.scalar.activation(out=tanh_b[:], in_=sum_b[:], func=ACT.Tanh)
-            weight = ring.tile([P, HALF], F32, name="weight")
-            nc.scalar.activation(out=weight[:], in_=wgs_sb[:, entries], func=ACT.Copy, scale=gain_sb[:, b, t : t + 1])
-            made[k] = (sum_a, tanh_b, weight)
+            made[k] = (sum_a, tanh_b)
 
         larger = {}
 
         def maximum(k):
-            sum_a, tanh_b, weight = made[k]
+            sum_a, tanh_b = made[k]
             larger[k] = ring.tile([P, HALF], F32, name="larger")
             nc.vector.tensor_tensor(larger[k][:], sum_a[:], tanh_b[:], ALU.max)
+
+        weights = {}
+
+        def weigh(k):
+            b, t, half = place(k)
+            if k == STEPS - 1:
+                weights[k] = ring.tile([P, HALF], F32, name="weight_last", tag="x_low", bufs=1, align_bytes=64)
+            else:
+                weights[k] = ring.tile([P, HALF], F32, name="weight")
+            nc.scalar.activation(
+                out=weights[k][:], in_=wgs_sb[:, half * HALF : (half + 1) * HALF], func=ACT.Copy,
+                scale=gain_sb[:, b, t : t + 1],
+            )
 
         def scatter(k):
             b, t, half = place(k)
             nc.vector.tensor_tensor(
                 pages[t][:].indirect(idx2[:, half * HALF // 16 : (half + 1) * HALF // 16]),
-                larger[k][:], made[k][2][:], ALU.mult,
+                larger[k][:], weights[k][:], ALU.mult,
             )
 
         x_first = {}
 
         def gather_first(t):
             x_first[t] = keep.tile([P, M], F32, name="x_first%d" % t, tag="x%d" % t, align_bytes=64)
-            nc.vector.tensor_tensor(x_first[t][:], pages[t][:].indirect(idx3[:]), wgt_neg[:], ALU.mult)
+            nc.vector.tensor_tensor(x_first[t][:], pages[t][:].indirect(idx3[:]), wgt_neg, ALU.mult)
 
         z0_q = held([P, M], U32, "z0_q")
         z0_s = held([P, M], U8, "z0_s")
@@ -250,69 +254,44 @@ def tile_list_pelt_round_scores_kernel(
                 in_=z_words[:].rearrange("p m u -> p (m u)").bitcast(BF16),
             )
 
-        side_jobs = {
-            0: prepare_wgt, 1: prepare_w1b, 2: lambda: round_w4(0), 3: load_w3,
-            4: lambda: round_w4(1), 5: lambda: load_light(0), 7: quantize_w4,
-        }
-        z_first = {}
-        products(0)
-        products(1)
-        maximum(0)
-        for k in range(STEPS):
-            if k + 2 < STEPS:
-                products(k + 2)
-            if k + 1 < STEPS:
-                maximum(k + 1)
-            if k % 2 == 0 and 2 <= k <= 2 * PACK:
-                gather_first(k // 2 - 1)
-            scatter(k)
-            if k in side_jobs:
-                side_jobs[k]()
-            c = k - (2 * PACK + 1)
-            if 0 <= c < CHUNKS:
-                z_first[c] = distance_first(c)
-            if 0 <= c - 1 < CHUNKS:
-                quantize_first(c - 1, z_first[c - 1])
-            if c == CHUNKS - 1:
-                load_light(1)
+        def span(c):
+            return slice(STARTS[c], STARTS[c] + WIDTHS[c])
 
-        x_second = {}
+        diff = {}
 
-        def gather_second(c, t):
-            if t == 0:
-                x_second[c] = keep.tile([P, PACK, CHUNK], F32, name="x_second", tag="x%d" % c, align_bytes=64)
-            nc.vector.tensor_tensor(
-                x_second[c][:, t, :], pages[t][:].indirect(idx3[:, c * CHUNK // 16 : (c + 1) * CHUNK // 16]),
-                wgt_neg[:, c * CHUNK : (c + 1) * CHUNK], ALU.mult,
-            )
-
-        z_second = {}
-
-        def distance_second(c):
-            diff = ring.tile([P, PACK, CHUNK], BF16, name="diff")
-            nc.vector.tensor_tensor(diff[:], x_second[c][:], light_sb[1][:, :, c * CHUNK : (c + 1) * CHUNK], ALU.add)
-            z_second[c] = ring.tile([P, CHUNK * PACK], BF16, name="z_second", align_bytes=64)
-            nc.scalar.activation(
-                out=z_second[c][:].rearrange("p (c i t) -> p c t i", i=4, t=PACK),
-                in_=diff[:].rearrange("p t (c i) -> p c t i", i=4), func=ACT.Abs,
-            )
+        def distance_pair(c, u):
+            cols = span(c)
+            x = ring.tile([P, 2, WIDTHS[c]], F32, name="x_pair", tag=("x_low", "turns")[u], bufs=1, align_bytes=64)
+            for e in range(2):
+                nc.vector.tensor_tensor(
+                    x[:, e, :], pages[2 * u + e][:].indirect(idx3[:, cols.start // 16 : cols.stop // 16]),
+                    wgt_neg[:, cols], ALU.mult,
+                )
+            if u == 0:
+                diff[c] = ring.tile([P, PACK, WIDTHS[c]], BF16, name="diff", bufs=2)
+            nc.vector.tensor_tensor(diff[c][:, 2 * u : 2 * u + 2, :], x[:], light_sb[1][:, 2 * u : 2 * u + 2, cols], ALU.add)
 
         z1 = {}
 
         def quantize_second(c):
-            z1_q = ring.tile([P, CHUNK], U32, name="z1_q", align_bytes=64)
-            z1_s = ring.tile([P, CHUNK], U8, name="z1_s", align_bytes=64)
-            nc.vector.quantize_mx(out=z1_q[:].bitcast(FP8X4), scales=z1_s[:], in_=z_second[c][:])
+            z_second = ring.tile([P, WIDTHS[c] * PACK], BF16, name="z_second", tag="turns", bufs=1, align_bytes=64)
+            nc.scalar.activation(
+                out=z_second[:].rearrange("p (c i t) -> p c t i", i=4, t=PACK),
+                in_=diff[c][:].rearrange("p t (c i) -> p c t i", i=4), func=ACT.Abs,
+            )
+            z1_q = ring.tile([P, WIDTHS[c]], U32, name="z1_q", align_bytes=64)
+            z1_s = ring.tile([P, WIDTHS[c]], U8, name="z1_s", align_bytes=64)
+            nc.vector.quantize_mx(out=z1_q[:].bitcast(FP8X4), scales=z1_s[:], in_=z_second[:])
             z1[c] = (z1_q, z1_s)
 
-        scored = {}
+        scored = []
 
-        def score(c, g):
-            tiles = GROUPS[g]
-            cols = slice(c * CHUNK, (c + 1) * CHUNK)
-            turn = (c * len(GROUPS) + g) % 2
-            y2 = psum.tile([P, len(tiles), CHUNK], F32, name="y2", tag="BR"[turn])
-            y = psum.tile([P, len(tiles), CHUNK], F32, name="y", tag="AF"[turn])
+        def score(c, tiles):
+            cols = span(c)
+            shape = [P, len(tiles), WIDTHS[c]]
+            turn = len(scored) % 2
+            y2 = psum.tile(shape, F32, name="y2", tag="BR"[turn])
+            y = psum.tile(shape, F32, name="y", tag="AF"[turn])
             moving = ((z0_q[:, cols], z0_s[:, cols]), (z1[c][0][:], z1[c][1][:]))
             for i, nt in enumerate(tiles):
                 for a in range(2):
@@ -325,49 +304,77 @@ def tile_list_pelt_round_scores_kernel(
                 for a in range(2):
                     wc = slice(nt * P, (nt + 1) * P)
                     nc.tensor.matmul_mx(
-                        out=y[:, i, :], lhsT=w3["q"][:, a, wc].bitcast(FP8X4), lhsT_scale=w3_s[:, a, wc],
+                        out=y[:, i, :], lhsT=w3_q[:, a, wc].bitcast(FP8X4), lhsT_scale=w3_s[:, a, wc],
                         rhs=moving[a][0].bitcast(FP8X4), rhs_scale=moving[a][1], start=(a == 0), stop=(a == 1),
                     )
-            size = ring.tile([P, len(tiles), CHUNK], F32, name="size", bufs=2)
+            size = ring.tile(shape, F32, name="size", tag="tanh_b")
             nc.scalar.activation(out=size[:], in_=y2[:], func=ACT.Abs)
-            root = ring.tile([P, len(tiles), CHUNK], F32, name="root", bufs=2)
+            root = ring.tile(shape, F32, name="root", tag="weight")
             nc.scalar.activation(out=root[:], in_=size[:], func=ACT.Abs_reciprocal_sqrt, bias=1.0)
-            inverse = ring.tile([P, len(tiles), CHUNK], F32, name="inverse")
-            nc.scalar.activation(out=inverse[:], in_=root[:], func=ACT.Square)
-            scored[c, g] = (y, inverse)
+            if c < SQUARED_CHUNKS:
+                inverse = ring.tile(shape, F32, name="inverse", tag="larger")
+                nc.scalar.activation(out=inverse[:], in_=root[:], func=ACT.Square)
+                scored.append((c, tiles, y, [inverse]))
+            else:
+                scored.append((c, tiles, y, [root, root]))
 
-        def finish(c, g):
-            tiles = GROUPS[g]
-            y, inverse = scored[c, g]
-            result = ring.tile([P, len(tiles), CHUNK], F32, name="result")
-            nc.vector.tensor_tensor(result[:], y[:], inverse[:], ALU.mult)
+        def finish(n):
+            c, tiles, value, factors_left = scored[n]
+            for factor in factors_left:
+                result = ring.tile([P, len(tiles), WIDTHS[c]], F32, name="result", bufs=6)
+                nc.vector.tensor_tensor(result[:], value[:], factor[:], ALU.mult)
+                value = result
             nc.sync.dma_start(
-                out=out[tiles[0] * P : (tiles[-1] + 1) * P, c * CHUNK : (c + 1) * CHUNK].rearrange("(i p) m -> p i m", p=P),
-                in_=result[:],
+                out=out[tiles[0] * P : (tiles[-1] + 1) * P, span(c)].rearrange("(i p) m -> p i m", p=P), in_=value[:]
             )
 
-        for t in range(PACK):
-            gather_second(0, t)
-        distance_second(0)
-        gather_second(1, 0)
-        gather_second(1, 1)
-        for c in range(CHUNKS):
-            quantize_second(c)
-            score(c, 0)
-            if c > 0:
-                finish(c - 1, 1)
-            if c + 1 < CHUNKS:
-                gather_second(c + 1, 2)
-                gather_second(c + 1, 3)
-            if c > 0:
-                finish(c - 1, 2)
-            if c + 1 < CHUNKS:
-                distance_second(c + 1)
-            score(c, 1)
-            score(c, 2)
-            finish(c, 0)
-            if c + 2 < CHUNKS:
-                gather_second(c + 2, 0)
-                gather_second(c + 2, 1)
-        finish(CHUNKS - 1, 1)
-        finish(CHUNKS - 1, 2)
+        side_jobs = {
+            0: lambda: nc.scalar.mul(wgt_neg, wgt_neg, -1.0), 1: lambda: quantize_w1(1, w1_raw1, 0),
+            3: lambda: round_w4(0), 5: lambda: round_w4(1), 7: quantize_w4,
+        }
+        z_first = {}
+        products(0)
+        weigh(0)
+        products(1)
+        maximum(0)
+        for k in range(STEPS):
+            if k + 2 < STEPS:
+                products(k + 2)
+            if k + 2 == STEPS:
+                distance_pair(0, 0)
+            if k + 1 < STEPS:
+                weigh(k + 1)
+            if k + 1 < STEPS:
+                maximum(k + 1)
+            if k % 2 == 0 and 2 <= k <= 2 * PACK:
+                gather_first(k // 2 - 1)
+            scatter(k)
+            if k in side_jobs:
+                side_jobs[k]()
+            c = k - (2 * PACK + 1)
+            if 0 <= c < CHUNKS:
+                z_first[c] = distance_first(c)
+            if 0 <= c - 1 < CHUNKS:
+                quantize_first(c - 1, z_first[c - 1])
+
+        last = len(WIDTHS) - 1
+        distance_pair(0, 1)
+        distance_pair(1, 0)
+        quantize_second(0)
+        finished = 0
+        for c in range(len(WIDTHS)):
+            score(c, GROUPS[0])
+            if c < last:
+                distance_pair(c + 1, 1)
+            while finished < len(scored) - 1:
+                finish(finished)
+                finished = finished + 1
+            if c + 1 < last:
+                distance_pair(c + 2, 0)
+            if c < last:
+                quantize_second(c + 1)
+            score(c, GROUPS[1])
+            score(c, GROUPS[2])
+        while finished < len(scored):
+            finish(finished)
+            finished = finished + 1

@@ -24,8 +24,9 @@ HALF = 512
 CHUNK = 256
 CHUNKS = M // CHUNK
 GROUPS = ((0, 1), (2, 3), (4,))
+NARROW = ((0, 1, 2, 3), (4,))
 STEPS = 2 * PACK * 2
-W1_ON_VECTOR = 48
+W1_ON_VECTOR = 0
 SQUARED_CHUNKS = 2
 WIDTHS = (128, 256, 256, 256, 128)
 STARTS = [sum(WIDTHS[:c]) for c in range(len(WIDTHS))]
@@ -88,10 +89,9 @@ def tile_list_pelt_round_scores_kernel(
                     in_=rounded[:, PACK * cols.start : PACK * cols.stop],
                 )
 
-        tab_w = held([P, T], I32, "tab_w", "big")
-        for cols in (slice(0, T // 2), slice(T // 2, T)):
-            nc.sync.dma_start(out=tab_w[:, cols], in_=tab_words[0].rearrange("p t i -> p (t i)").bitcast(I32)[:, cols])
         w1_raw0 = load_rows(held([P, PACK * K_PASS], F32, "w1_raw0", "late")[:], w1[:, :K_PASS])
+        tab_w = held([P, T], I32, "tab_w", "big")
+        nc.sync.dma_start(out=tab_w[:], in_=tab_words[0].rearrange("p t i -> p (t i)").bitcast(I32))
         load_scale_rows(nc.scalar, tab_s, tab_scales)
 
         pages = [held([P, T2], F32, "page%d" % t) for t in range(2)]
@@ -124,9 +124,12 @@ def tile_list_pelt_round_scores_kernel(
                     gathered[half][:], window.indirect(idx[:, half * HALF // 16 : (half + 1) * HALF // 16])
                 )
         quantize_w1(0, w1_raw0, W1_ON_VECTOR)
-        for t, tag in ((2, "tab_s"), (3, "big")):
-            pages.append(held([P, T2], F32, "page%d" % t, tag))
-            nc.gpsimd.memset(pages[t][:], 0.0)
+
+        def add_page(tag):
+            pages.append(held([P, T2], F32, "page%d" % len(pages), tag))
+            nc.gpsimd.memset(pages[-1][:], 0.0)
+
+        add_page("w1_bf0")
 
         identity = held([P, P], F32, "identity")
         make_identity(nc, identity[:])
@@ -140,11 +143,14 @@ def tile_list_pelt_round_scores_kernel(
         light_sb = [load_rows(parts[2], light[:K_PASS, :])]
         w4_raw = [load_rows(parts[3 + a], w4[a * K_PASS : (a + 1) * K_PASS, :]) for a in range(2)]
         light_sb.append(load_rows(parts[5], light[K_PASS:, :]))
-        w3_q = held([P, 2, N], I32, "w3_q", "w1_bf0")
+        w3_q = held([P, 2, N], I32, "w3_q", "big")
         nc.sync.dma_start(out=w3_q[:], in_=w3_words.rearrange("a p c i -> p a (c i)").bitcast(I32))
-        w3_s = held([P, 2, N], U8, "w3_s", "w2_s_raw")
-        nc.gpsimd.memset(w3_s[:].bitcast(I32), 0)
-        load_scale_rows(nc.sync, w3_s, w3_scales)
+        w3_s = []
+
+        def load_w3_scales():
+            w3_s.append(held([P, 2, N], U8, "w3_s", "w1_s0"))
+            nc.gpsimd.memset(w3_s[0][:].bitcast(I32), 0)
+            load_scale_rows(nc.sync, w3_s[0], w3_scales)
 
         w4_q = held([P, 2 * N], U32, "w4_q")
         w4_s = held([P, 2 * N], U8, "w4_s")
@@ -189,15 +195,20 @@ def tile_list_pelt_round_scores_kernel(
 
         def maximum(k):
             sum_a, tanh_b = made[k]
-            larger[k] = ring.tile([P, HALF], F32, name="larger")
+            if k == 1:
+                larger[k] = ring.tile([P, HALF], F32, name="larger_second", tag="first", bufs=1)
+            else:
+                larger[k] = ring.tile([P, HALF], F32, name="larger")
             nc.vector.tensor_tensor(larger[k][:], sum_a[:], tanh_b[:], ALU.max)
 
         weights = {}
 
         def weigh(k):
             b, t, half = place(k)
-            if k == STEPS - 1:
-                weights[k] = ring.tile([P, HALF], F32, name="weight_last", tag="x_low", bufs=1, align_bytes=64)
+            if k == 0:
+                weights[k] = ring.tile([P, HALF], F32, name="weight_first", tag="first", bufs=1)
+            elif k == STEPS - 1:
+                weights[k] = ring.tile([P, HALF], F32, name="weight_last", tag="x_pair", bufs=2, align_bytes=64)
             else:
                 weights[k] = ring.tile([P, HALF], F32, name="weight")
             nc.scalar.activation(
@@ -259,22 +270,27 @@ def tile_list_pelt_round_scores_kernel(
 
         diff = {}
 
-        def distance_pair(c, u):
+        x_pairs = {}
+
+        def gather_pair(c, u):
             cols = span(c)
-            x = ring.tile([P, 2, WIDTHS[c]], F32, name="x_pair", tag=("x_low", "turns")[u], bufs=1, align_bytes=64)
+            x_pairs[c, u] = ring.tile([P, 2, WIDTHS[c]], F32, name="x_pair", tag="x_pair", bufs=2, align_bytes=64)
             for e in range(2):
                 nc.vector.tensor_tensor(
-                    x[:, e, :], pages[2 * u + e][:].indirect(idx3[:, cols.start // 16 : cols.stop // 16]),
+                    x_pairs[c, u][:, e, :], pages[2 * u + e][:].indirect(idx3[:, cols.start // 16 : cols.stop // 16]),
                     wgt_neg[:, cols], ALU.mult,
                 )
+
+        def subtract_pair(c, u):
             if u == 0:
-                diff[c] = ring.tile([P, PACK, WIDTHS[c]], BF16, name="diff", bufs=2)
-            nc.vector.tensor_tensor(diff[c][:, 2 * u : 2 * u + 2, :], x[:], light_sb[1][:, 2 * u : 2 * u + 2, cols], ALU.add)
+                diff[c] = ring.tile([P, PACK, WIDTHS[c]], BF16, name="diff", bufs=1)
+            slices = slice(2 * u, 2 * u + 2)
+            nc.vector.tensor_tensor(diff[c][:, slices, :], x_pairs[c, u][:], light_sb[1][:, slices, span(c)], ALU.add)
 
         z1 = {}
 
         def quantize_second(c):
-            z_second = ring.tile([P, WIDTHS[c] * PACK], BF16, name="z_second", tag="turns", bufs=1, align_bytes=64)
+            z_second = ring.tile([P, WIDTHS[c] * PACK], BF16, name="z_second", bufs=2, align_bytes=64)
             nc.scalar.activation(
                 out=z_second[:].rearrange("p (c i t) -> p c t i", i=4, t=PACK),
                 in_=diff[c][:].rearrange("p t (c i) -> p c t i", i=4), func=ACT.Abs,
@@ -304,7 +320,7 @@ def tile_list_pelt_round_scores_kernel(
                 for a in range(2):
                     wc = slice(nt * P, (nt + 1) * P)
                     nc.tensor.matmul_mx(
-                        out=y[:, i, :], lhsT=w3_q[:, a, wc].bitcast(FP8X4), lhsT_scale=w3_s[:, a, wc],
+                        out=y[:, i, :], lhsT=w3_q[:, a, wc].bitcast(FP8X4), lhsT_scale=w3_s[0][:, a, wc],
                         rhs=moving[a][0].bitcast(FP8X4), rhs_scale=moving[a][1], start=(a == 0), stop=(a == 1),
                     )
             size = ring.tile(shape, F32, name="size", tag="tanh_b")
@@ -330,7 +346,8 @@ def tile_list_pelt_round_scores_kernel(
 
         side_jobs = {
             0: lambda: nc.scalar.mul(wgt_neg, wgt_neg, -1.0), 1: lambda: quantize_w1(1, w1_raw1, 0),
-            3: lambda: round_w4(0), 5: lambda: round_w4(1), 7: quantize_w4,
+            2: lambda: add_page("w1_bf1"), 3: lambda: round_w4(0), 5: lambda: round_w4(1), 7: quantize_w4,
+            8: load_w3_scales,
         }
         z_first = {}
         products(0)
@@ -341,14 +358,21 @@ def tile_list_pelt_round_scores_kernel(
             if k + 2 < STEPS:
                 products(k + 2)
             if k + 2 == STEPS:
-                distance_pair(0, 0)
+                gather_pair(0, 0)
+                subtract_pair(0, 0)
             if k + 1 < STEPS:
                 weigh(k + 1)
+            if k == 0:
+                scatter(0)
             if k + 1 < STEPS:
                 maximum(k + 1)
+            if k + 3 == STEPS:
+                warm = held([P, 1], F32, "warm")
+                nc.scalar.activation(out=warm[:], in_=made[k + 2][1][:, :1], func=ACT.Abs_reciprocal_sqrt, bias=2.0)
             if k % 2 == 0 and 2 <= k <= 2 * PACK:
                 gather_first(k // 2 - 1)
-            scatter(k)
+            if k > 0:
+                scatter(k)
             if k in side_jobs:
                 side_jobs[k]()
             c = k - (2 * PACK + 1)
@@ -358,23 +382,27 @@ def tile_list_pelt_round_scores_kernel(
                 quantize_first(c - 1, z_first[c - 1])
 
         last = len(WIDTHS) - 1
-        distance_pair(0, 1)
-        distance_pair(1, 0)
+        gather_pair(0, 1)
+        subtract_pair(0, 1)
+        gather_pair(1, 0)
         quantize_second(0)
         finished = 0
         for c in range(len(WIDTHS)):
-            score(c, GROUPS[0])
+            groups = GROUPS if WIDTHS[c] == CHUNK else NARROW
+            score(c, groups[0])
             if c < last:
-                distance_pair(c + 1, 1)
+                subtract_pair(c + 1, 0)
+                gather_pair(c + 1, 1)
+                subtract_pair(c + 1, 1)
             while finished < len(scored) - 1:
                 finish(finished)
                 finished = finished + 1
             if c + 1 < last:
-                distance_pair(c + 2, 0)
+                gather_pair(c + 2, 0)
             if c < last:
                 quantize_second(c + 1)
-            score(c, GROUPS[1])
-            score(c, GROUPS[2])
+            for tiles in groups[1:]:
+                score(c, tiles)
         while finished < len(scored):
             finish(finished)
             finished = finished + 1

from contextlib import ExitStack

import concourse.mybir as mybir
from concourse.masks import make_identity

K, H, N, T, S, M, T2 = 512, 1024, 640, 4096, 1024, 1024, 2048
FLOPS = 2 * (2 * K * H * S + 2 * H * N * M)

F32 = mybir.dt.float32
BF16 = mybir.dt.bfloat16
I32 = mybir.dt.int32
U32 = mybir.dt.uint32
U16 = mybir.dt.uint16
U8 = mybir.dt.uint8
FP8X4 = mybir.dt.float8_e4m3fn_x4
FP4X4 = mybir.dt.float4_e2m1fn_x4
ALU = mybir.AluOpType
ACT = mybir.ActivationFunctionType

P = 128
PACK = 4
K_PASS = P * PACK
HALF = 512
CHUNK = 256
CHUNKS = M // CHUNK
GROUPS = ((0, 1), (2, 3), (4,))
NARROW = ((0, 1, 2, 3), (4,))
STEPS = 2 * PACK * 2
W1_ON_VECTOR = 0
SQUARED_CHUNKS = 2
WIDTHS = (128, 256, 256, 256, 128)
STARTS = [sum(WIDTHS[:c]) for c in range(len(WIDTHS))]


def tile_list_pelt_round_scores_kernel(
    tc, tab_words, tab_scales, offs, offs2, offs3, w1, w2_words, w2_scales, gain, wgs, wgt, light,
    w3_words, w3_scales, w4, out,
):
    nc = tc.nc
    with ExitStack() as ctx:
        lists = ctx.enter_context(tc.tile_pool(name="lists", bufs=1))
        keep = ctx.enter_context(tc.tile_pool(name="keep", bufs=1))
        ring = ctx.enter_context(tc.tile_pool(name="ring", bufs=3))
        psum = ctx.enter_context(tc.psum_pool(name="psum", bufs=2))

        def held(shape, dtype, name, tag=None):
            return keep.tile(shape, dtype, name=name, tag=tag or name, align_bytes=64)

        def load_scale_rows(engine, plane, rows):
            for q in range(4):
                engine.dma_start(
                    out=plane[32 * q : 32 * q + 4].bitcast(I32),
                    in_=rows[:, 4 * q : 4 * q + 4, :].rearrange("a r c -> r a c").bitcast(I32),
                )

        tab_s = held([P, 1, T], U8, "tab_s", "tab_s")
        nc.vector.memset(tab_s[:].bitcast(I32), 0)
        w2_s_raw = held([P, 1, H], U8, "w2_s_raw", "w2_s_raw")
        nc.gpsimd.memset(w2_s_raw[:].bitcast(I32), 0)
        load_scale_rows(nc.gpsimd, w2_s_raw, w2_scales)

        idx = lists.tile([P, S // 16], U16, name="idx")
        nc.sync.dma_start(idx[:], offs)
        idx2 = lists.tile([P, S // 16], U16, name="idx2")
        nc.sync.dma_start(idx2[:], offs2)
        idx3 = lists.tile([P, M // 16], U16, name="idx3")
        nc.sync.dma_start(idx3[:], offs3)
        w2_raw = held([P, 2 * H], U8, "w2_raw", "w2_raw")
        nc.sync.dma_start(out=w2_raw[:].bitcast(I32), in_=w2_words[0].bitcast(I32))

        w1_q = [held([P, K_PASS], U32, "w1_q%d" % b) for b in range(2)]
        w1_s = [held([P, K_PASS], U8, "w1_s%d" % b) for b in range(2)]

        def load_rows(flat, rows):
            raw = flat.rearrange("p (j c) -> p j c", j=PACK)
            nc.sync.dma_start(out=raw, in_=rows.rearrange("(p j) c -> p j c", j=PACK))
            return raw

        def quantize_w1(b, raw, on_vector):
            rounded = held([P, PACK * K_PASS], BF16, "w1_bf%d" % b)
            dealt = rounded[:].rearrange("p (t m j) -> p m j t", t=PACK, j=PACK)
            source = raw.rearrange("p j (m t) -> p m j t", t=PACK)
            nc.scalar.copy(out=dealt[:, on_vector:], in_=source[:, on_vector:])
            if on_vector:
                nc.vector.tensor_copy(out=dealt[:, :on_vector], in_=source[:, :on_vector])
            for cols in (slice(0, 2 * P), slice(2 * P, 4 * P)):
                nc.vector.quantize_mx(
                    out=w1_q[b][:, cols].bitcast(FP8X4), scales=w1_s[b][:, cols],
                    in_=rounded[:, PACK * cols.start : PACK * cols.stop],
                )

        w1_raw0 = load_rows(held([P, PACK * K_PASS], F32, "w1_raw0", "late")[:], w1[:, :K_PASS])
        tab_w = held([P, T], I32, "tab_w", "big")
        nc.sync.dma_start(out=tab_w[:], in_=tab_words[0].rearrange("p t i -> p (t i)").bitcast(I32))
        load_scale_rows(nc.scalar, tab_s, tab_scales)

        pages = [held([P, T2], F32, "page%d" % t) for t in range(2)]
        for page in pages:
            nc.vector.memset(page[:], 0.0)

        w2_q = held([P, 2 * H], U8, "w2_q")
        for b in range(2):
            cols = slice(b * H, (b + 1) * H)
            nc.vector.tensor_copy(
                out=w2_q[:, cols].bitcast(U16).rearrange("p (t m) -> p t m", t=PACK),
                in_=w2_raw[:, cols].bitcast(U16).rearrange("p (m t) -> p t m", t=PACK),
            )
        w2_s = held([P, H], U8, "w2_s")
        nc.vector.tensor_copy(
            out=w2_s[:].rearrange("p (b t m) -> p b t m", b=2, t=PACK),
            in_=w2_s_raw[:, 0, :].rearrange("p (b m t) -> p b t m", b=2, t=PACK),
        )
        factors = held([P, S + 2 * PACK], F32, "factors", "w2_raw")
        wgs_sb = factors[:, :S]
        gain_sb = factors[:, S:].rearrange("p (b t) -> p b t", b=2)
        nc.sync.dma_start(out=gain_sb, in_=gain.rearrange("(b p t) -> p b t", b=2, t=PACK))
        nc.sync.dma_start(out=wgs_sb, in_=wgs)

        v_s = [held([P, HALF], U8, "v_s%d" % half) for half in range(2)]
        v_q = [held([P, HALF], U32, "v_q%d" % half) for half in range(2)]
        for gathered, window in ((v_s, tab_s[:, 0, :]), (v_q, tab_w[:].bitcast(U32))):
            for half in range(2):
                nc.vector.tensor_copy(
                    gathered[half][:], window.indirect(idx[:, half * HALF // 16 : (half + 1) * HALF // 16])
                )
        quantize_w1(0, w1_raw0, W1_ON_VECTOR)

        def add_page(tag):
            pages.append(held([P, T2], F32, "page%d" % len(pages), tag))
            nc.gpsimd.memset(pages[-1][:], 0.0)

        add_page("w1_bf0")

        identity = held([P, P], F32, "identity")
        make_identity(nc, identity[:])

        sizes = [M, PACK * K_PASS, PACK * M, PACK * N, PACK * N, PACK * M]
        late = held([P, sum(sizes)], F32, "late", "late")
        parts = [late[:, sum(sizes[:n]) : sum(sizes[: n + 1])] for n in range(len(sizes))]
        wgt_neg = parts[0]
        nc.sync.dma_start(out=wgt_neg, in_=wgt)
        w1_raw1 = load_rows(parts[1], w1[:, K_PASS:])
        light_sb = [load_rows(parts[2], light[:K_PASS, :])]
        w4_raw = [load_rows(parts[3 + a], w4[a * K_PASS : (a + 1) * K_PASS, :]) for a in range(2)]
        light_sb.append(load_rows(parts[5], light[K_PASS:, :]))
        w3_q = held([P, 2, N], I32, "w3_q", "big")
        nc.sync.dma_start(out=w3_q[:], in_=w3_words.rearrange("a p c i -> p a (c i)").bitcast(I32))
        w3_s = []

        def load_w3_scales():
            w3_s.append(held([P, 2, N], U8, "w3_s", "w1_s0"))
            nc.gpsimd.memset(w3_s[0][:].bitcast(I32), 0)
            load_scale_rows(nc.sync, w3_s[0], w3_scales)

        w4_q = held([P, 2 * N], U32, "w4_q")
        w4_s = held([P, 2 * N], U8, "w4_s")
        w4_bf = held([P, 2 * N * PACK], BF16, "w4_bf")

        def round_w4(a):
            nc.scalar.copy(
                out=w4_bf[:, a * N * PACK : (a + 1) * N * PACK].rearrange("p (c i j) -> p c j i", i=4, j=PACK),
                in_=w4_raw[a].rearrange("p j (c i) -> p c j i", i=4),
            )

        def quantize_w4():
            for lo, hi in ((0, 1024), (1024, 2 * N)):
                nc.vector.quantize_mx(
                    out=w4_q[:, lo:hi].bitcast(FP8X4), scales=w4_s[:, lo:hi], in_=w4_bf[:, PACK * lo : PACK * hi]
                )

        def place(k):
            return k // (2 * PACK), k // 2 % PACK, k % 2

        made = {}

        def products(k):
            b, t, half = place(k)
            cols = slice(t * P, (t + 1) * P)
            sum_b = psum.tile([P, HALF], F32, name="sum_b", tag="B")
            c2 = b * K_PASS + t * P
            nc.tensor.matmul_mx(
                out=sum_b[:], lhsT=w2_q[:, 2 * c2 : 2 * (c2 + P)].bitcast(FP4X4), lhsT_scale=w2_s[:, c2 : c2 + P],
                rhs=v_q[half][:].bitcast(FP8X4), rhs_scale=v_s[half][:], start=True, stop=True,
            )
            sum_a = psum.tile([P, HALF], F32, name="sum_a", tag="A")
            nc.tensor.matmul_mx(
                out=sum_a[:], lhsT=w1_q[b][:, cols].bitcast(FP8X4), lhsT_scale=w1_s[b][:, cols],
                rhs=v_q[half][:].bitcast(FP8X4), rhs_scale=v_s[half][:], start=True, stop=True,
            )
            tanh_b = ring.tile([P, HALF], F32, name="tanh_b")
            nc.scalar.activation(out=tanh_b[:], in_=sum_b[:], func=ACT.Tanh)
            made[k] = (sum_a, tanh_b)

        larger = {}

        def maximum(k):
            sum_a, tanh_b = made[k]
            if k == 1:
                larger[k] = ring.tile([P, HALF], F32, name="larger_second", tag="first", bufs=1)
            else:
                larger[k] = ring.tile([P, HALF], F32, name="larger")
            nc.vector.tensor_tensor(larger[k][:], sum_a[:], tanh_b[:], ALU.max)

        weights = {}

        def weigh(k):
            b, t, half = place(k)
            if k == 0:
                weights[k] = ring.tile([P, HALF], F32, name="weight_first", tag="first", bufs=1)
            elif k == STEPS - 1:
                weights[k] = ring.tile([P, HALF], F32, name="weight_last", tag="x_pair", bufs=2, align_bytes=64)
            else:
                weights[k] = ring.tile([P, HALF], F32, name="weight")
            nc.scalar.activation(
                out=weights[k][:], in_=wgs_sb[:, half * HALF : (half + 1) * HALF], func=ACT.Copy,
                scale=gain_sb[:, b, t : t + 1],
            )

        def scatter(k):
            b, t, half = place(k)
            nc.vector.tensor_tensor(
                pages[t][:].indirect(idx2[:, half * HALF // 16 : (half + 1) * HALF // 16]),
                larger[k][:], weights[k][:], ALU.mult,
            )

        x_first = {}

        def gather_first(t):
            x_first[t] = keep.tile([P, M], F32, name="x_first%d" % t, tag="x%d" % t, align_bytes=64)
            nc.vector.tensor_tensor(x_first[t][:], pages[t][:].indirect(idx3[:]), wgt_neg, ALU.mult)

        z0_q = held([P, M], U32, "z0_q")
        z0_s = held([P, M], U8, "z0_s")

        def distance_first(c):
            back = psum.tile([P, 2, CHUNK], F32, name="back", tag="R")
            for u in range(2):
                turned = psum.tile([P, 2, 2, P], F32, name="turned", tag="F")
                blocks = [(a, e) for a in range(2) for e in range(2)]
                for n, (a, e) in enumerate(blocks):
                    cols = slice(c * CHUNK + a * P, c * CHUNK + (a + 1) * P)
                    nc.tensor.matmul(
                        turned[:, a, e, :], light_sb[0][:, 2 * u + e, cols], identity[:],
                        start=(n == 0), stop=False, is_transpose=True,
                    )
                for n, (a, e) in enumerate(blocks):
                    cols = slice(c * CHUNK + a * P, c * CHUNK + (a + 1) * P)
                    nc.tensor.matmul(
                        turned[:, a, e, :], x_first[2 * u + e][:, cols], identity[:],
                        start=False, stop=(n == len(blocks) - 1), is_transpose=True,
                    )
                pairs = ring.tile([P, 2, P, 2], BF16, name="pairs")
                nc.scalar.activation(out=pairs[:], in_=turned[:].rearrange("m a e p -> m a p e"), func=ACT.Abs)
                words = pairs[:].rearrange("m a p e -> m (a p e)").bitcast(F32)
                for a in range(2):
                    nc.tensor.transpose(back[:, u, a * P : (a + 1) * P], words[:, a * P : (a + 1) * P], identity[:])
            z_words = ring.tile([P, CHUNK, 2], F32, name="z_words", align_bytes=64)
            nc.scalar.copy(out=z_words[:], in_=back[:].rearrange("p u m -> p m u"))
            return z_words

        def quantize_first(c, z_words):
            cols = slice(c * CHUNK, (c + 1) * CHUNK)
            nc.vector.quantize_mx(
                out=z0_q[:, cols].bitcast(FP8X4), scales=z0_s[:, cols],
                in_=z_words[:].rearrange("p m u -> p (m u)").bitcast(BF16),
            )

        def span(c):
            return slice(STARTS[c], STARTS[c] + WIDTHS[c])

        diff = {}

        x_pairs = {}

        def gather_pair(c, u):
            cols = span(c)
            x_pairs[c, u] = ring.tile([P, 2, WIDTHS[c]], F32, name="x_pair", tag="x_pair", bufs=2, align_bytes=64)
            for e in range(2):
                nc.vector.tensor_tensor(
                    x_pairs[c, u][:, e, :], pages[2 * u + e][:].indirect(idx3[:, cols.start // 16 : cols.stop // 16]),
                    wgt_neg[:, cols], ALU.mult,
                )

        def subtract_pair(c, u):
            if u == 0:
                diff[c] = ring.tile([P, PACK, WIDTHS[c]], BF16, name="diff", bufs=1)
            slices = slice(2 * u, 2 * u + 2)
            nc.vector.tensor_tensor(diff[c][:, slices, :], x_pairs[c, u][:], light_sb[1][:, slices, span(c)], ALU.add)

        z1 = {}

        def quantize_second(c):
            z_second = ring.tile([P, WIDTHS[c] * PACK], BF16, name="z_second", bufs=2, align_bytes=64)
            nc.scalar.activation(
                out=z_second[:].rearrange("p (c i t) -> p c t i", i=4, t=PACK),
                in_=diff[c][:].rearrange("p t (c i) -> p c t i", i=4), func=ACT.Abs,
            )
            z1_q = ring.tile([P, WIDTHS[c]], U32, name="z1_q", align_bytes=64)
            z1_s = ring.tile([P, WIDTHS[c]], U8, name="z1_s", align_bytes=64)
            nc.vector.quantize_mx(out=z1_q[:].bitcast(FP8X4), scales=z1_s[:], in_=z_second[:])
            z1[c] = (z1_q, z1_s)

        scored = []

        def score(c, tiles):
            cols = span(c)
            shape = [P, len(tiles), WIDTHS[c]]
            turn = len(scored) % 2
            y2 = psum.tile(shape, F32, name="y2", tag="BR"[turn])
            y = psum.tile(shape, F32, name="y", tag="AF"[turn])
            moving = ((z0_q[:, cols], z0_s[:, cols]), (z1[c][0][:], z1[c][1][:]))
            for i, nt in enumerate(tiles):
                for a in range(2):
                    wc = slice(a * N + nt * P, a * N + (nt + 1) * P)
                    nc.tensor.matmul_mx(
                        out=y2[:, i, :], lhsT=w4_q[:, wc].bitcast(FP8X4), lhsT_scale=w4_s[:, wc],
                        rhs=moving[a][0].bitcast(FP8X4), rhs_scale=moving[a][1], start=(a == 0), stop=(a == 1),
                    )
            for i, nt in enumerate(tiles):
                for a in range(2):
                    wc = slice(nt * P, (nt + 1) * P)
                    nc.tensor.matmul_mx(
                        out=y[:, i, :], lhsT=w3_q[:, a, wc].bitcast(FP8X4), lhsT_scale=w3_s[0][:, a, wc],
                        rhs=moving[a][0].bitcast(FP8X4), rhs_scale=moving[a][1], start=(a == 0), stop=(a == 1),
                    )
            size = ring.tile(shape, F32, name="size", tag="tanh_b")
            nc.scalar.activation(out=size[:], in_=y2[:], func=ACT.Abs)
            root = ring.tile(shape, F32, name="root", tag="weight")
            nc.scalar.activation(out=root[:], in_=size[:], func=ACT.Abs_reciprocal_sqrt, bias=1.0)
            if c < SQUARED_CHUNKS:
                inverse = ring.tile(shape, F32, name="inverse", tag="larger")
                nc.scalar.activation(out=inverse[:], in_=root[:], func=ACT.Square)
                scored.append((c, tiles, y, [inverse]))
            else:
                scored.append((c, tiles, y, [root, root]))

        def finish(n):
            c, tiles, value, factors_left = scored[n]
            for factor in factors_left:
                result = ring.tile([P, len(tiles), WIDTHS[c]], F32, name="result", bufs=6)
                nc.vector.tensor_tensor(result[:], value[:], factor[:], ALU.mult)
                value = result
            nc.sync.dma_start(
                out=out[tiles[0] * P : (tiles[-1] + 1) * P, span(c)].rearrange("(i p) m -> p i m", p=P), in_=value[:]
            )

        side_jobs = {
            0: lambda: nc.scalar.mul(wgt_neg, wgt_neg, -1.0), 1: lambda: quantize_w1(1, w1_raw1, 0),
            2: lambda: add_page("w1_bf1"), 3: lambda: round_w4(0), 5: lambda: round_w4(1), 7: quantize_w4,
            8: load_w3_scales,
        }
        z_first = {}
        products(0)
        weigh(0)
        products(1)
        maximum(0)
        for k in range(STEPS):
            if k + 2 < STEPS:
                products(k + 2)
            if k + 2 == STEPS:
                gather_pair(0, 0)
                subtract_pair(0, 0)
            if k + 1 < STEPS:
                weigh(k + 1)
            if k == 0:
                scatter(0)
            if k + 1 < STEPS:
                maximum(k + 1)
            if k + 3 == STEPS:
                warm = held([P, 1], F32, "warm")
                nc.scalar.activation(out=warm[:], in_=made[k + 2][1][:, :1], func=ACT.Abs_reciprocal_sqrt, bias=2.0)
            if k % 2 == 0 and 2 <= k <= 2 * PACK:
                gather_first(k // 2 - 1)
            if k > 0:
                scatter(k)
            if k in side_jobs:
                side_jobs[k]()
            c = k - (2 * PACK + 1)
            if 0 <= c < CHUNKS:
                z_first[c] = distance_first(c)
            if 0 <= c - 1 < CHUNKS:
                quantize_first(c - 1, z_first[c - 1])

        last = len(WIDTHS) - 1
        gather_pair(0, 1)
        subtract_pair(0, 1)
        gather_pair(1, 0)
        quantize_second(0)
        finished = 0
        for c in range(len(WIDTHS)):
            groups = GROUPS if WIDTHS[c] == CHUNK else NARROW
            score(c, groups[0])
            if c < last:
                subtract_pair(c + 1, 0)
                gather_pair(c + 1, 1)
                subtract_pair(c + 1, 1)
            while finished < len(scored) - 1:
                finish(finished)
                finished = finished + 1
            if c + 1 < last:
                gather_pair(c + 2, 0)
            if c < last:
                quantize_second(c + 1)
            for tiles in groups[1:]:
                score(c, tiles)
        while finished < len(scored):
            finish(finished)
            finished = finished + 1
